import numpy as np
import ml_dtypes


def mxq(x, axis, fmt="e4m3"):
    dtype, down = {"e4m3": (ml_dtypes.float8_e4m3fn, 7), "e5m2": (ml_dtypes.float8_e5m2, 14)}[fmt]
    v = np.moveaxis(np.asarray(x, np.float32).astype(ml_dtypes.bfloat16).astype(np.float64), axis, -1)
    blocks = v.reshape(v.shape[:-1] + (-1, 32))
    amax = np.abs(blocks).max(-1, keepdims=True)
    byte = np.maximum(np.where(amax > 0, np.frexp(amax)[1] - 1 + 127, 0) - down, 1)
    scale = np.exp2(byte - 127.0)
    codes = (blocks / scale).astype(np.float32).astype(dtype).astype(np.float64)
    return np.moveaxis((codes * scale).reshape(v.shape), -1, axis)


WIDE = False


def mx_kscale(k):
    if not WIDE:
        return np.ones(k)
    levels = np.array([10, -10, 5, -5, 0])
    if k % 512:
        return np.exp2(np.random.permutation(np.resize(levels, k // 32))).repeat(32)
    a = np.empty((k // 512, 16))
    for p in range(k // 512):
        a[p, :8] = np.random.permutation(np.resize(levels, 8))
        for g in range(8):
            far = levels[np.abs(levels - a[p, g]) >= 10]
            a[p, g + 8] = far[np.random.randint(len(far))]
    return np.exp2(a.ravel()).repeat(32)


def f64(x):
    return np.asarray(x).astype(np.float64)


def striped(idx):
    return np.tile(idx.reshape(-1, 16).T, (8, 1)).astype(np.uint16)


def unstriped(offs):
    return offs[:16].T.reshape(-1).astype(np.int64)


def striped8(idx):
    return np.concatenate([x.reshape(-1, 16).T for x in idx]).astype(np.uint16)


def runs(offs, k):
    lists = np.stack([offs[16 * r : 16 * r + 16].T.reshape(-1) for r in range(8)]).astype(np.int64)
    return lists[np.arange(k) % 512 // 64]


def pack_weight(w):
    k, n = w.shape
    w = f64(np.asarray(w, np.float32).astype(ml_dtypes.bfloat16)).reshape(k // 32, 32, n)
    amax = np.abs(w).max(1)
    byte = np.clip(np.where(amax > 0, np.frexp(amax)[1] - 1 + 127 - 7, 1), 1, 254)
    scaled = (w * np.exp2(127.0 - byte)[:, None, :]).reshape(k, n).astype(np.float32)
    words = np.ascontiguousarray(scaled.reshape(k // 512, 128, 4, n).transpose(0, 1, 3, 2)).astype(ml_dtypes.float8_e4m3fn).view(np.uint8)
    return words, np.ascontiguousarray(byte.astype(np.uint8).reshape(k // 512, 16, n))


def unpack_weight(words, scales):
    g, p, n, _ = words.shape
    vals = np.ascontiguousarray(words).view(ml_dtypes.float8_e4m3fn).astype(np.float64) * np.repeat(np.exp2(scales.astype(np.float64) - 127.0), 8, axis=1)[..., None]
    return vals.transpose(0, 1, 3, 2).reshape(g * 512, n)


def relu(v):
    return np.maximum(v, 0.0)

def planes(y):
    n, m = y.shape
    v = y.astype(np.float32).astype(ml_dtypes.bfloat16).astype(np.float64).reshape(n // 32, 32, m)
    top = np.abs(v).max(1)
    byte = np.clip(np.where(top > 0, np.frexp(top)[1] - 1 + 127 - 7, 1), 1, 254)
    codes = (v * np.exp2(127.0 - byte)[:, None, :]).reshape(n, m).astype(np.float32).astype(ml_dtypes.float8_e4m3fn).view(np.uint8)
    words = codes.reshape(n // 512, 128, 4, m).transpose(0, 1, 3, 2)
    return np.ascontiguousarray(words), np.ascontiguousarray(byte.astype(np.uint8).reshape(n // 512, 16, m))


K, T, S, G, H, W, C = 512, 1024, 256, 2048, 512, 128, 512


def setup_inputs():
    n = np.random.standard_normal
    s = mx_kscale(K)[:, None]
    packed_xT = pack_weight(n((K, T)) * s)
    packed_dT = pack_weight(n((K, G)) / s)
    return {
        "x_words": packed_xT[0],
        "x_scales": packed_xT[1],
        "d_words": packed_dT[0],
        "d_scales": packed_dT[1],
        "gs": (np.random.uniform(0.5, 1.5, (K, 1)) / s).astype(np.float32),
        "offs": striped(np.random.permutation(T)[:S]),
        "ka": striped8(np.random.randint(0, G, (8, H))),
        "kb": striped8(np.random.randint(0, G, (8, H))),
        "n1": striped(np.random.permutation(S)[:W]),
        "n2": striped(np.random.permutation(S)[:W]),
        "n3": striped(np.random.permutation(S)),
        "cand": striped(np.random.permutation(T)[:C]),
        "n4": striped(np.random.permutation(S)),
    }


def reference(x_words, x_scales, d_words, d_scales, gs, offs, ka, kb, n1, n2, n3, cand, n4):
    x_cand = unpack_weight(x_words, x_scales)[:, unstriped(cand)]
    d_ka = unpack_weight(d_words, d_scales)[np.arange(K)[:, None], runs(ka, K)]
    xq = unpack_weight(x_words, x_scales)[:, unstriped(offs)]
    d_kb = unpack_weight(d_words, d_scales)[np.arange(K)[:, None], runs(kb, K)]
    h = 0.0625 * (d_ka.T @ xq + d_kb.T @ xq)
    pa = h[:, unstriped(n2)]
    ds = h.copy()
    ds[:, unstriped(n1)] = pa
    z = f64(gs) * (ds - (0.5 * ds[:, unstriped(n3)]))
    s = 0.0625 * ((x_cand.T @ mxq(z, 0, "e4m3")))
    rl = relu(s)
    ds2 = np.zeros((C, S))
    ds2[:, unstriped(n4)] = rl
    out_0 = ds2 - (0.5 * s)
    return (out_0,) + planes(out_0)

@@ -1,0 +1,230 @@
+from contextlib import ExitStack
+
+import concourse.mybir as mybir
+from concourse.masks import make_identity
+
+K, T, S, G, H, W, C = 512, 1024, 256, 2048, 512, 128, 512
+FLOPS = 2 * K * S * (H + H + C)
+
+F32 = mybir.dt.float32
+BF16 = mybir.dt.bfloat16
+I32 = mybir.dt.int32
+U32 = mybir.dt.uint32
+U16 = mybir.dt.uint16
+U8 = mybir.dt.uint8
+FP8X4 = mybir.dt.float8_e4m3fn_x4
+ALU = mybir.AluOpType
+COPY = mybir.ActivationFunctionType.Copy
+
+P = 128
+PACK = 4
+TILES = 4
+HALF = 128
+PAIR = 256
+LANES = 16
+
+
+def tile_picked_aqcksetsend_none_po_kernel(
+    tc, x_words, x_scales, d_words, d_scales, gs, offs, ka, kb, n1, n2, n3, cand, n4, out_0, out_1, out_2
+):
+    nc = tc.nc
+    with ExitStack() as ctx:
+        keep = ctx.enter_context(tc.tile_pool(name="keep", bufs=1))
+        psum = ctx.enter_context(tc.psum_pool(name="psum", bufs=1))
+
+        def load_list(src, name):
+            lst = keep.tile(list(src.shape), U16, name=name)
+            nc.sync.dma_start(lst[:], src)
+            return lst
+
+        def entries(lst, start, count):
+            return lst[:, start // LANES : (start + count) // LANES]
+
+        d_sc = keep.tile([P, G], U8, name="d_sc", align_bytes=64)
+        x_sc = keep.tile([P, T], U8, name="x_sc", align_bytes=64)
+        nc.vector.memset(d_sc[:].bitcast(I32), 0)
+        nc.gpsimd.memset(x_sc[:].bitcast(I32), 0)
+
+        ka_l = load_list(ka, "ka_l")
+        gs_t = keep.tile([P, TILES], F32, name="gs_t")
+        with nc.allow_non_contiguous_dma(reason="one weight for each partition and row tile"):
+            nc.scalar.dma_start(gs_t[:], gs.rearrange("(t p) o -> p (t o)", p=P))
+        kb_l = load_list(kb, "kb_l")
+        offs_l = load_list(offs, "offs_l")
+        nc.sync.dma_start(d_sc[0:P:8, :].bitcast(I32), d_scales[0].bitcast(I32))
+        nc.sync.dma_start(x_sc[0:P:8, :].bitcast(I32), x_scales[0].bitcast(I32))
+        d_w = keep.tile([P, G], I32, name="d_w", align_bytes=64)
+        nc.sync.dma_start(d_w[:], d_words[0].rearrange("p n t -> p (n t)").bitcast(I32))
+        x_w = keep.tile([P, T], I32, name="x_w", align_bytes=64)
+        nc.sync.dma_start(x_w[:], x_words[0].rearrange("p n t -> p (n t)").bitcast(I32))
+
+        all_planes = keep.tile([P, 2 * H + S + C], U8, name="all_planes", align_bytes=64)
+        nc.gpsimd.memset(all_planes[:].bitcast(I32), 0)
+        planes = [all_planes[:, 0 : 2 * PAIR + S], all_planes[:, 2 * PAIR + S : 2 * H + S]]
+        c_plane = all_planes[:, 2 * H + S :]
+        ident = keep.tile([P, P], F32, name="ident")
+        make_identity(nc, ident[:])
+        ident_bf = keep.tile([P, P], BF16, name="ident_bf")
+        nc.gpsimd.tensor_copy(ident_bf[:], ident[:])
+        gs16 = []
+        for pair in range(2):
+            gs16.append(keep.tile([P, 2], F32, name="gs16_%d" % pair, tag="gs16_0" if pair == 0 else "late"))
+            nc.scalar.activation(gs16[pair][:], gs_t[:, 2 * pair : 2 * pair + 2], COPY, scale=0.0625)
+
+        def place_scale_rows(gathered, plane, queues):
+            for r in range(4):
+                queues[r % len(queues)].dma_start(plane[r:P:32, :].bitcast(I32), gathered[8 * r : P : 32, :].bitcast(I32))
+
+        ds = []
+        xq_w = keep.tile([P, S], U32, name="xq_w", align_bytes=64)
+        for pair in range(2):
+            first = pair * PAIR
+            width = 2 * PAIR + (S if pair == 0 else 0)
+            got = keep.tile([P, width], U8, name="got%d" % pair, tag="got", align_bytes=64)
+            nc.vector.tensor_copy(got[:, 0:PAIR], d_sc[:].indirect(entries(ka_l, first, PAIR)))
+            nc.vector.tensor_copy(got[:, PAIR : 2 * PAIR], d_sc[:].indirect(entries(kb_l, first, PAIR)))
+            if pair == 0:
+                nc.vector.tensor_copy(got[:, 2 * PAIR :], x_sc[:].indirect(offs_l[:]))
+            plane = planes[pair]
+            place_scale_rows(got, plane, (nc.sync, nc.scalar) if pair == 0 else (nc.sync,))
+            if pair == 0:
+                n2_l = load_list(n2, "n2_l")
+                n1_l = load_list(n1, "n1_l")
+                n3_l = load_list(n3, "n3_l")
+                cand_l = load_list(cand, "cand_l")
+                n4_l = load_list(n4, "n4_l")
+            xq_sc = planes[0][:, 2 * PAIR :]
+            if pair == 0:
+                ka_w = keep.tile([P, PAIR], U32, name="ka_w0", tag="words_a", align_bytes=64)
+                kb_w = keep.tile([P, PAIR], U32, name="kb_w0", tag="words_b", align_bytes=64)
+            else:
+                both_w = keep.tile([P, 2 * PAIR], U32, name="both_w1", tag="words_a", align_bytes=64)
+                ka_w, kb_w = both_w[:, 0:PAIR], both_w[:, PAIR:]
+            nc.vector.tensor_copy(ka_w[:], d_w[:].bitcast(U32).indirect(entries(ka_l, first, PAIR)))
+            nc.vector.tensor_copy(kb_w[:], d_w[:].bitcast(U32).indirect(entries(kb_l, first, PAIR)))
+            if pair == 0:
+                nc.vector.tensor_copy(xq_w[:], x_w[:].bitcast(U32).indirect(offs_l[:]))
+            for e in range(2):
+                t = 2 * pair + e
+                acc = psum.tile([P, S], F32, name="h_ps%d" % t, tag="acc%d" % t)
+                for which, words in enumerate((ka_w, kb_w)):
+                    nc.tensor.matmul_mx(
+                        out=acc[:],
+                        lhsT=words[:, e * P : (e + 1) * P].bitcast(FP8X4),
+                        lhsT_scale=plane[:, which * PAIR + e * P : which * PAIR + (e + 1) * P],
+                        rhs=xq_w[:].bitcast(FP8X4),
+                        rhs_scale=xq_sc,
+                        start=(which == 0),
+                        stop=(which == 1),
+                    )
+                window = keep.tile([P, S], F32, name="ds%d" % t)
+                if pair == 0:
+                    nc.scalar.activation(window[:], acc[:], COPY, scale=gs16[pair][:, e : e + 1])
+                else:
+                    nc.vector.tensor_scalar(window[:], acc[:], gs16[pair][:, e : e + 1], None, ALU.mult)
+                ds.append(window)
+
+        c_got = keep.tile([P, TILES, P], U8, name="c_got", tag="words_b", align_bytes=64)
+        nc.vector.tensor_copy(c_got[:].rearrange("p t m -> p m t"), x_sc[:].indirect(cand_l[:]))
+        place_scale_rows(c_got[:].rearrange("p t m -> p (t m)"), c_plane, (nc.sync,))
+        c_w = keep.tile([P, TILES, P], U32, name="c_w", tag="words_a", align_bytes=64)
+        nc.vector.tensor_copy(c_w[:].rearrange("p t m -> p m t"), x_w[:].bitcast(U32).indirect(cand_l[:]))
+
+        zt_first = psum.tile([P, H - P], F32, name="zt_first", tag="acc3")
+        zt_last = psum.tile([P, P], F32, name="zt_last")
+        zb = [keep.tile([P, 2, P, 2], BF16, name="zb0", align_bytes=64)]
+
+        def add_transpose(t, src, start, stop):
+            dst = zt_first[:, t * P : (t + 1) * P] if t < TILES - 1 else zt_last[:]
+            nc.tensor.matmul(dst, src, ident[:], start=start, stop=stop, is_transpose=True)
+
+        def round_rows(hf, t0, t1, turned):
+            nc.vector.tensor_copy(
+                zb[hf][:, :, 32 * t0 : 32 * t1, :], turned.rearrange("j (a u e) -> j u a e", u=2, e=2)
+            )
+
+        for pair in range(2):
+            tiles = (2 * pair, 2 * pair + 1)
+            pa = keep.tile([P, 2, W], F32, name="pa%d" % pair, tag="pa0" if pair == 0 else "late")
+            for t in tiles:
+                nc.scalar.activation(pa[:, t % 2, :], ds[t][:].indirect(n2_l[:]), COPY)
+            for t in tiles:
+                nc.scalar.activation(ds[t][:].indirect(n1_l[:]), pa[:, t % 2, :], COPY)
+            for t in tiles:
+                other = keep.tile([P, HALF], F32, name="other_a%d" % t, tag="other_a%d" % t)
+                nc.scalar.activation(other[:], ds[t][:].indirect(entries(n3_l, 0, HALF)), COPY, scale=-0.5)
+                add_transpose(t, ds[t][:, 0:HALF], True, False)
+                add_transpose(t, other[:], False, True)
+                if t == 1:
+                    round_rows(0, 0, 2, zt_first[:, 0 : 2 * P])
+                if t == 2:
+                    round_rows(0, 2, 3, zt_first[:, 2 * P :])
+        round_rows(0, TILES - 1, TILES, zt_last[:])
+
+        other_b = keep.tile([P, TILES, HALF], F32, name="other_b", tag="late")
+        z_b = keep.tile([P, TILES, HALF], BF16, name="z_b")
+        for t in range(TILES):
+            nc.scalar.activation(other_b[:, t, :], ds[t][:].indirect(entries(n3_l, HALF, HALF)), COPY, scale=-0.5)
+            nc.gpsimd.tensor_tensor(z_b[:, t, :], ds[t][:, HALF:S], other_b[:, t, :], ALU.add)
+
+        s_ps = [psum.tile([P, S], F32, name="s_ps%d" % t, tag="acc%d" % t) for t in range(TILES)]
+        ds2 = [keep.tile([P, S], F32, name="ds2_%d" % t) for t in range(TILES)]
+        for hf in range(2):
+            cols = slice(hf * HALF, (hf + 1) * HALF)
+            if hf == 1:
+                zt_b = psum.tile([P, H], BF16, name="zt_b", tag="back0")
+                for t in range(TILES):
+                    nc.tensor.transpose(zt_b[:, t * P : (t + 1) * P], z_b[:, t, :], ident_bf[:])
+                zb.append(keep.tile([P, 2, P, 2], BF16, name="zb1", tag="z_w0", align_bytes=64))
+                round_rows(1, 0, TILES, zt_b[:])
+            back = psum.tile([P, 2, HALF], F32, name="back%d" % hf, tag="back%d" % hf)
+            words = zb[hf][:].rearrange("j u p e -> j (u p e)").bitcast(F32)
+            for u in range(2):
+                nc.tensor.transpose(back[:, u, :], words[:, u * P : (u + 1) * P], ident[:])
+            z_in = keep.tile([P, HALF * PACK], BF16, name="z_in%d" % hf, align_bytes=64)
+            nc.vector.tensor_copy(
+                z_in[:].bitcast(F32).rearrange("p (j u) -> p j u", u=2), back[:].rearrange("p u j -> p j u")
+            )
+            z_w = keep.tile([P, HALF], U32, name="z_w%d" % hf, tag="z_w%d" % hf, align_bytes=64)
+            z_sc = keep.tile([P, HALF], U8, name="z_sc%d" % hf, align_bytes=64)
+            nc.vector.quantize_mx(out=z_w[:].bitcast(FP8X4), scales=z_sc[:], in_=z_in[:])
+            for t in range(TILES):
+                nc.tensor.matmul_mx(
+                    out=s_ps[t][:, cols],
+                    lhsT=c_w[:, t, :].bitcast(FP8X4),
+                    lhsT_scale=c_plane[:, t * P : (t + 1) * P],
+                    rhs=z_w[:].bitcast(FP8X4),
+                    rhs_scale=z_sc[:],
+                    start=True,
+                    stop=True,
+                )
+                rl = keep.tile([P, HALF], F32, name="rl%d_%d" % (hf, t))
+                nc.vector.tensor_scalar(rl[:], s_ps[t][:, cols], 0.0625, 0.0, ALU.mult, ALU.max)
+                nc.scalar.activation(ds2[t][:].indirect(entries(n4_l, hf * HALF, HALF)), rl[:], COPY)
+
+        y = keep.tile([P, TILES, S], F32, name="y")
+        y_rows = out_0.rearrange("(p t) j -> p t j", t=PACK)
+        for t in range(TILES):
+            parts = (slice(0, S),) if t < TILES - 1 else (slice(0, HALF), slice(HALF, S))
+            for cols in parts:
+                nc.vector.scalar_tensor_tensor(
+                    y[:, t, cols], s_ps[t][:, cols], -0.03125, ds2[t][:, cols], ALU.mult, ALU.add
+                )
+            nc.sync.dma_start(y_rows[:, t, :], y[:, t, :])
+
+        y_w = keep.tile([P, S], U32, name="y_w", align_bytes=64)
+        y_sc = keep.tile([P, S], U8, name="y_sc", align_bytes=64)
+        y_in = [keep.tile([P, HALF * PACK], BF16, name="y_in%d" % hf, align_bytes=64) for hf in range(2)]
+        for hf in range(2):
+            cols = slice(hf * HALF, (hf + 1) * HALF)
+            nc.vector.tensor_copy(
+                y_in[hf][:].rearrange("p (c i t) -> p c t i", i=4, t=PACK),
+                y[:, :, cols].rearrange("p t (c i) -> p c t i", i=4),
+            )
+        for hf in range(2):
+            cols = slice(hf * HALF, (hf + 1) * HALF)
+            nc.vector.quantize_mx(out=y_w[:, cols].bitcast(FP8X4), scales=y_sc[:, cols], in_=y_in[hf][:])
+        nc.sync.dma_start(out_1[0].rearrange("p n t -> p (n t)").bitcast(I32), y_w[:].bitcast(I32))
+        for q in range(4):
+            queue = nc.scalar if q % 2 == 0 else nc.sync
+            queue.dma_start(out_2[0, 4 * q : 4 * q + 4, :].bitcast(I32), y_sc[32 * q : 32 * q + 4, :].bitcast(I32))

@@ -42,30 +42,32 @@ def tile_picked_aqcksetsend_none_po_kernel(
 
         d_sc = keep.tile([P, G], U8, name="d_sc", align_bytes=64)
         x_sc = keep.tile([P, T], U8, name="x_sc", align_bytes=64)
+        nc.vector.memset(x_sc[:].bitcast(I32), 0)
         nc.vector.memset(d_sc[:].bitcast(I32), 0)
-        nc.gpsimd.memset(x_sc[:].bitcast(I32), 0)
 
-        ka_l = load_list(ka, "ka_l")
-        gs_t = keep.tile([P, TILES], F32, name="gs_t")
-        with nc.allow_non_contiguous_dma(reason="one weight for each partition and row tile"):
-            nc.scalar.dma_start(gs_t[:], gs.rearrange("(t p) o -> p (t o)", p=P))
-        kb_l = load_list(kb, "kb_l")
         offs_l = load_list(offs, "offs_l")
-        nc.sync.dma_start(d_sc[0:P:8, :].bitcast(I32), d_scales[0].bitcast(I32))
         nc.sync.dma_start(x_sc[0:P:8, :].bitcast(I32), x_scales[0].bitcast(I32))
+        ka_l = load_list(ka, "ka_l")
+        nc.sync.dma_start(d_sc[0:P:8, :].bitcast(I32), d_scales[0].bitcast(I32))
+        kb_l = load_list(kb, "kb_l")
         d_w = keep.tile([P, G], I32, name="d_w", align_bytes=64)
         nc.sync.dma_start(d_w[:], d_words[0].rearrange("p n t -> p (n t)").bitcast(I32))
         x_w = keep.tile([P, T], I32, name="x_w", align_bytes=64)
         nc.sync.dma_start(x_w[:], x_words[0].rearrange("p n t -> p (n t)").bitcast(I32))
-
+        ident = keep.tile([P, P], F32, name="ident")
+        nc.vector.memset(ident[:], 0.0)
+        make_identity(nc, ident[:], nomemset=True)
+        gs_rows = keep.tile([P, P], F32, name="gs_rows")
+        nc.vector.memset(gs_rows[:], 0.0)
+        nc.sync.dma_start(gs_rows[0:TILES, :], gs.rearrange("(t p) o -> t (p o)", p=P))
+        gs_t = psum.tile([P, P], F32, name="gs_t")
+        nc.tensor.transpose(gs_t[:], gs_rows[:], ident[:])
         all_planes = keep.tile([P, 2 * H + S + C], U8, name="all_planes", align_bytes=64)
-        nc.gpsimd.memset(all_planes[:].bitcast(I32), 0)
+        nc.vector.memset(all_planes[:].bitcast(I32), 0)
         planes = [all_planes[:, 0 : 2 * PAIR + S], all_planes[:, 2 * PAIR + S : 2 * H + S]]
         c_plane = all_planes[:, 2 * H + S :]
-        ident = keep.tile([P, P], F32, name="ident")
-        make_identity(nc, ident[:])
         ident_bf = keep.tile([P, P], BF16, name="ident_bf")
-        nc.gpsimd.tensor_copy(ident_bf[:], ident[:])
+        nc.scalar.activation(ident_bf[:], ident[:], COPY)
         gs16 = []
         for pair in range(2):
             gs16.append(keep.tile([P, 2], F32, name="gs16_%d" % pair, tag="gs16_0" if pair == 0 else "late"))
@@ -81,12 +83,12 @@ def tile_picked_aqcksetsend_none_po_kernel(
             first = pair * PAIR
             width = 2 * PAIR + (S if pair == 0 else 0)
             got = keep.tile([P, width], U8, name="got%d" % pair, tag="got", align_bytes=64)
-            nc.vector.tensor_copy(got[:, 0:PAIR], d_sc[:].indirect(entries(ka_l, first, PAIR)))
-            nc.vector.tensor_copy(got[:, PAIR : 2 * PAIR], d_sc[:].indirect(entries(kb_l, first, PAIR)))
             if pair == 0:
                 nc.vector.tensor_copy(got[:, 2 * PAIR :], x_sc[:].indirect(offs_l[:]))
+            nc.vector.tensor_copy(got[:, 0:PAIR], d_sc[:].indirect(entries(ka_l, first, PAIR)))
+            nc.vector.tensor_copy(got[:, PAIR : 2 * PAIR], d_sc[:].indirect(entries(kb_l, first, PAIR)))
             plane = planes[pair]
-            place_scale_rows(got, plane, (nc.sync, nc.scalar) if pair == 0 else (nc.sync,))
+            place_scale_rows(got, plane, (nc.sync,))
             if pair == 0:
                 n2_l = load_list(n2, "n2_l")
                 n1_l = load_list(n1, "n1_l")

@@ -50,10 +50,10 @@ def tile_picked_aqcksetsend_none_po_kernel(
         ka_l = load_list(ka, "ka_l")
         nc.sync.dma_start(d_sc[0:P:8, :].bitcast(I32), d_scales[0].bitcast(I32))
         kb_l = load_list(kb, "kb_l")
-        d_w = keep.tile([P, G], I32, name="d_w", align_bytes=64)
-        nc.sync.dma_start(d_w[:], d_words[0].rearrange("p n t -> p (n t)").bitcast(I32))
         x_w = keep.tile([P, T], I32, name="x_w", align_bytes=64)
         nc.sync.dma_start(x_w[:], x_words[0].rearrange("p n t -> p (n t)").bitcast(I32))
+        d_w = keep.tile([P, G], I32, name="d_w", align_bytes=64)
+        nc.sync.dma_start(d_w[:], d_words[0].rearrange("p n t -> p (n t)").bitcast(I32))
         ident = keep.tile([P, P], F32, name="ident")
         nc.vector.memset(ident[:], 0.0)
         make_identity(nc, ident[:], nomemset=True)
@@ -82,7 +82,7 @@ def tile_picked_aqcksetsend_none_po_kernel(
         for pair in range(2):
             first = pair * PAIR
             width = 2 * PAIR + (S if pair == 0 else 0)
-            got = keep.tile([P, width], U8, name="got%d" % pair, tag="got", align_bytes=64)
+            got = keep.tile([P, width], U8, name="got%d" % pair, align_bytes=64)
             if pair == 0:
                 nc.vector.tensor_copy(got[:, 2 * PAIR :], x_sc[:].indirect(offs_l[:]))
             nc.vector.tensor_copy(got[:, 0:PAIR], d_sc[:].indirect(entries(ka_l, first, PAIR)))
@@ -97,21 +97,16 @@ def tile_picked_aqcksetsend_none_po_kernel(
                 n4_l = load_list(n4, "n4_l")
             xq_sc = planes[0][:, 2 * PAIR :]
             if pair == 0:
-                ka_w = keep.tile([P, PAIR], U32, name="ka_w0", tag="words_a", align_bytes=64)
-                kb_w = keep.tile([P, PAIR], U32, name="kb_w0", tag="words_b", align_bytes=64)
-            else:
-                both_w = keep.tile([P, 2 * PAIR], U32, name="both_w1", tag="words_a", align_bytes=64)
-                ka_w, kb_w = both_w[:, 0:PAIR], both_w[:, PAIR:]
+                nc.vector.tensor_copy(xq_w[:], x_w[:].bitcast(U32).indirect(offs_l[:]))
+            ka_w = keep.tile([P, PAIR], U32, name="ka_w%d" % pair, tag="ka_w%d" % pair, align_bytes=64)
+            kb_w = keep.tile([P, PAIR], U32, name="kb_w%d" % pair, tag="kb_w%d" % pair, align_bytes=64)
             nc.vector.tensor_copy(ka_w[:], d_w[:].bitcast(U32).indirect(entries(ka_l, first, PAIR)))
             nc.vector.tensor_copy(kb_w[:], d_w[:].bitcast(U32).indirect(entries(kb_l, first, PAIR)))
-            if pair == 0:
-                nc.vector.tensor_copy(xq_w[:], x_w[:].bitcast(U32).indirect(offs_l[:]))
-            for e in range(2):
-                t = 2 * pair + e
-                acc = psum.tile([P, S], F32, name="h_ps%d" % t, tag="acc%d" % t)
-                for which, words in enumerate((ka_w, kb_w)):
+            accs = [psum.tile([P, S], F32, name="h_ps%d" % t, tag="acc%d" % t) for t in (2 * pair, 2 * pair + 1)]
+            for which, words in enumerate((ka_w, kb_w)):
+                for e in range(2):
                     nc.tensor.matmul_mx(
-                        out=acc[:],
+                        out=accs[e][:],
                         lhsT=words[:, e * P : (e + 1) * P].bitcast(FP8X4),
                         lhsT_scale=plane[:, which * PAIR + e * P : which * PAIR + (e + 1) * P],
                         rhs=xq_w[:].bitcast(FP8X4),
@@ -119,22 +114,23 @@ def tile_picked_aqcksetsend_none_po_kernel(
                         start=(which == 0),
                         stop=(which == 1),
                     )
-                window = keep.tile([P, S], F32, name="ds%d" % t)
+            for e in range(2):
+                window = keep.tile([P, S], F32, name="ds%d" % (2 * pair + e))
                 if pair == 0:
-                    nc.scalar.activation(window[:], acc[:], COPY, scale=gs16[pair][:, e : e + 1])
+                    nc.scalar.activation(window[:], accs[e][:], COPY, scale=gs16[pair][:, e : e + 1])
                 else:
-                    nc.vector.tensor_scalar(window[:], acc[:], gs16[pair][:, e : e + 1], None, ALU.mult)
+                    nc.vector.tensor_scalar(window[:], accs[e][:], gs16[pair][:, e : e + 1], None, ALU.mult)
                 ds.append(window)
 
-        c_got = keep.tile([P, TILES, P], U8, name="c_got", tag="words_b", align_bytes=64)
+        c_got = keep.tile([P, TILES, P], U8, name="c_got", tag="kb_w0", align_bytes=64)
         nc.vector.tensor_copy(c_got[:].rearrange("p t m -> p m t"), x_sc[:].indirect(cand_l[:]))
         place_scale_rows(c_got[:].rearrange("p t m -> p (t m)"), c_plane, (nc.sync,))
-        c_w = keep.tile([P, TILES, P], U32, name="c_w", tag="words_a", align_bytes=64)
+        c_w = keep.tile([P, TILES, P], U32, name="c_w", tag="kb_w1", align_bytes=64)
         nc.vector.tensor_copy(c_w[:].rearrange("p t m -> p m t"), x_w[:].bitcast(U32).indirect(cand_l[:]))
 
         zt_first = psum.tile([P, H - P], F32, name="zt_first", tag="acc3")
         zt_last = psum.tile([P, P], F32, name="zt_last")
-        zb = [keep.tile([P, 2, P, 2], BF16, name="zb0", align_bytes=64)]
+        zb = [keep.tile([P, 2, P, 2], BF16, name="zb0", tag="zb0", align_bytes=64)]
 
         def add_transpose(t, src, start, stop):
             dst = zt_first[:, t * P : (t + 1) * P] if t < TILES - 1 else zt_last[:]
@@ -164,19 +160,22 @@ def tile_picked_aqcksetsend_none_po_kernel(
         round_rows(0, TILES - 1, TILES, zt_last[:])
 
         other_b = keep.tile([P, TILES, HALF], F32, name="other_b", tag="late")
-        z_b = keep.tile([P, TILES, HALF], BF16, name="z_b")
         for t in range(TILES):
             nc.scalar.activation(other_b[:, t, :], ds[t][:].indirect(entries(n3_l, HALF, HALF)), COPY, scale=-0.5)
-            nc.gpsimd.tensor_tensor(z_b[:, t, :], ds[t][:, HALF:S], other_b[:, t, :], ALU.add)
 
         s_ps = [psum.tile([P, S], F32, name="s_ps%d" % t, tag="acc%d" % t) for t in range(TILES)]
         ds2 = [keep.tile([P, S], F32, name="ds2_%d" % t) for t in range(TILES)]
         for hf in range(2):
             cols = slice(hf * HALF, (hf + 1) * HALF)
             if hf == 1:
+                z_first = keep.tile([P, TILES - 1, HALF], BF16, name="z_first", tag="other_a3")
+                z_last = keep.tile([P, HALF], BF16, name="z_last", tag="zb0", align_bytes=64)
+                z_b = [z_first[:, t, :] for t in range(TILES - 1)] + [z_last[:]]
+                for t in range(TILES):
+                    nc.vector.tensor_tensor(z_b[t], ds[t][:, HALF:S], other_b[:, t, :], ALU.add)
                 zt_b = psum.tile([P, H], BF16, name="zt_b", tag="back0")
                 for t in range(TILES):
-                    nc.tensor.transpose(zt_b[:, t * P : (t + 1) * P], z_b[:, t, :], ident_bf[:])
+                    nc.tensor.transpose(zt_b[:, t * P : (t + 1) * P], z_b[t], ident_bf[:])
                 zb.append(keep.tile([P, 2, P, 2], BF16, name="zb1", tag="z_w0", align_bytes=64))
                 round_rows(1, 0, TILES, zt_b[:])
             back = psum.tile([P, 2, HALF], F32, name="back%d" % hf, tag="back%d" % hf)

from contextlib import ExitStack

import concourse.mybir as mybir
from concourse.masks import make_identity

K, T, S, G, H, W, C = 512, 1024, 256, 2048, 512, 128, 512
FLOPS = 2 * K * S * (H + H + C)

F32 = mybir.dt.float32
BF16 = mybir.dt.bfloat16
I32 = mybir.dt.int32
U32 = mybir.dt.uint32
U16 = mybir.dt.uint16
U8 = mybir.dt.uint8
FP8X4 = mybir.dt.float8_e4m3fn_x4
ALU = mybir.AluOpType
COPY = mybir.ActivationFunctionType.Copy

P = 128
PACK = 4
TILES = 4
HALF = 128
PAIR = 256
LANES = 16


def tile_picked_aqcksetsend_none_po_kernel(
    tc, x_words, x_scales, d_words, d_scales, gs, offs, ka, kb, n1, n2, n3, cand, n4, out_0, out_1, out_2
):
    nc = tc.nc
    with ExitStack() as ctx:
        keep = ctx.enter_context(tc.tile_pool(name="keep", bufs=1))
        psum = ctx.enter_context(tc.psum_pool(name="psum", bufs=1))

        def load_list(src, name):
            lst = keep.tile(list(src.shape), U16, name=name)
            nc.sync.dma_start(lst[:], src)
            return lst

        def entries(lst, start, count):
            return lst[:, start // LANES : (start + count) // LANES]

        d_sc = keep.tile([P, G], U8, name="d_sc", align_bytes=64)
        x_sc = keep.tile([P, T], U8, name="x_sc", align_bytes=64)
        nc.vector.memset(x_sc[:].bitcast(I32), 0)
        nc.vector.memset(d_sc[:].bitcast(I32), 0)

        offs_l = load_list(offs, "offs_l")
        nc.sync.dma_start(x_sc[0:P:8, :].bitcast(I32), x_scales[0].bitcast(I32))
        ka_l = load_list(ka, "ka_l")
        nc.sync.dma_start(d_sc[0:P:8, :].bitcast(I32), d_scales[0].bitcast(I32))
        kb_l = load_list(kb, "kb_l")
        x_w = keep.tile([P, T], I32, name="x_w", align_bytes=64)
        nc.sync.dma_start(x_w[:], x_words[0].rearrange("p n t -> p (n t)").bitcast(I32))
        d_w = keep.tile([P, G], I32, name="d_w", align_bytes=64)
        nc.sync.dma_start(d_w[:], d_words[0].rearrange("p n t -> p (n t)").bitcast(I32))
        ident = keep.tile([P, P], F32, name="ident")
        nc.vector.memset(ident[:], 0.0)
        make_identity(nc, ident[:], nomemset=True)
        gs_rows = keep.tile([P, P], F32, name="gs_rows")
        nc.vector.memset(gs_rows[:], 0.0)
        nc.sync.dma_start(gs_rows[0:TILES, :], gs.rearrange("(t p) o -> t (p o)", p=P))
        gs_t = psum.tile([P, P], F32, name="gs_t")
        nc.tensor.transpose(gs_t[:], gs_rows[:], ident[:])
        all_planes = keep.tile([P, 2 * H + S + C], U8, name="all_planes", align_bytes=64)
        nc.vector.memset(all_planes[:].bitcast(I32), 0)
        planes = [all_planes[:, 0 : 2 * PAIR + S], all_planes[:, 2 * PAIR + S : 2 * H + S]]
        c_plane = all_planes[:, 2 * H + S :]
        ident_bf = keep.tile([P, P], BF16, name="ident_bf")
        nc.scalar.activation(ident_bf[:], ident[:], COPY)
        gs16 = []
        for pair in range(2):
            gs16.append(keep.tile([P, 2], F32, name="gs16_%d" % pair, tag="gs16_0" if pair == 0 else "late"))
            nc.scalar.activation(gs16[pair][:], gs_t[:, 2 * pair : 2 * pair + 2], COPY, scale=0.0625)

        def place_scale_rows(gathered, plane, queues):
            for r in range(4):
                queues[r % len(queues)].dma_start(plane[r:P:32, :].bitcast(I32), gathered[8 * r : P : 32, :].bitcast(I32))

        ds = []
        xq_w = keep.tile([P, S], U32, name="xq_w", align_bytes=64)
        for pair in range(2):
            first = pair * PAIR
            width = 2 * PAIR + (S if pair == 0 else 0)
            got = keep.tile([P, width], U8, name="got%d" % pair, align_bytes=64)
            if pair == 0:
                nc.vector.tensor_copy(got[:, 2 * PAIR :], x_sc[:].indirect(offs_l[:]))
            nc.vector.tensor_copy(got[:, 0:PAIR], d_sc[:].indirect(entries(ka_l, first, PAIR)))
            nc.vector.tensor_copy(got[:, PAIR : 2 * PAIR], d_sc[:].indirect(entries(kb_l, first, PAIR)))
            plane = planes[pair]
            place_scale_rows(got, plane, (nc.sync,))
            if pair == 0:
                n2_l = load_list(n2, "n2_l")
                n1_l = load_list(n1, "n1_l")
                n3_l = load_list(n3, "n3_l")
                cand_l = load_list(cand, "cand_l")
                n4_l = load_list(n4, "n4_l")
            xq_sc = planes[0][:, 2 * PAIR :]
            if pair == 0:
                nc.vector.tensor_copy(xq_w[:], x_w[:].bitcast(U32).indirect(offs_l[:]))
            ka_w = keep.tile([P, PAIR], U32, name="ka_w%d" % pair, tag="ka_w%d" % pair, align_bytes=64)
            kb_w = keep.tile([P, PAIR], U32, name="kb_w%d" % pair, tag="kb_w%d" % pair, align_bytes=64)
            nc.vector.tensor_copy(ka_w[:], d_w[:].bitcast(U32).indirect(entries(ka_l, first, PAIR)))
            nc.vector.tensor_copy(kb_w[:], d_w[:].bitcast(U32).indirect(entries(kb_l, first, PAIR)))
            accs = [psum.tile([P, S], F32, name="h_ps%d" % t, tag="acc%d" % t) for t in (2 * pair, 2 * pair + 1)]
            for which, words in enumerate((ka_w, kb_w)):
                for e in range(2):
                    nc.tensor.matmul_mx(
                        out=accs[e][:],
                        lhsT=words[:, e * P : (e + 1) * P].bitcast(FP8X4),
                        lhsT_scale=plane[:, which * PAIR + e * P : which * PAIR + (e + 1) * P],
                        rhs=xq_w[:].bitcast(FP8X4),
                        rhs_scale=xq_sc,
                        start=(which == 0),
                        stop=(which == 1),
                    )
            for e in range(2):
                window = keep.tile([P, S], F32, name="ds%d" % (2 * pair + e))
                if pair == 0:
                    nc.scalar.activation(window[:], accs[e][:], COPY, scale=gs16[pair][:, e : e + 1])
                else:
                    nc.vector.tensor_scalar(window[:], accs[e][:], gs16[pair][:, e : e + 1], None, ALU.mult)
                ds.append(window)

        c_got = keep.tile([P, TILES, P], U8, name="c_got", tag="kb_w0", align_bytes=64)
        nc.vector.tensor_copy(c_got[:].rearrange("p t m -> p m t"), x_sc[:].indirect(cand_l[:]))
        place_scale_rows(c_got[:].rearrange("p t m -> p (t m)"), c_plane, (nc.sync,))
        c_w = keep.tile([P, TILES, P], U32, name="c_w", tag="kb_w1", align_bytes=64)
        nc.vector.tensor_copy(c_w[:].rearrange("p t m -> p m t"), x_w[:].bitcast(U32).indirect(cand_l[:]))

        zt_first = psum.tile([P, H - P], F32, name="zt_first", tag="acc3")
        zt_last = psum.tile([P, P], F32, name="zt_last")
        zb = [keep.tile([P, 2, P, 2], BF16, name="zb0", tag="zb0", align_bytes=64)]

        def add_transpose(t, src, start, stop):
            dst = zt_first[:, t * P : (t + 1) * P] if t < TILES - 1 else zt_last[:]
            nc.tensor.matmul(dst, src, ident[:], start=start, stop=stop, is_transpose=True)

        def round_rows(hf, t0, t1, turned):
            nc.vector.tensor_copy(
                zb[hf][:, :, 32 * t0 : 32 * t1, :], turned.rearrange("j (a u e) -> j u a e", u=2, e=2)
            )

        for pair in range(2):
            tiles = (2 * pair, 2 * pair + 1)
            pa = keep.tile([P, 2, W], F32, name="pa%d" % pair, tag="pa0" if pair == 0 else "late")
            for t in tiles:
                nc.scalar.activation(pa[:, t % 2, :], ds[t][:].indirect(n2_l[:]), COPY)
            for t in tiles:
                nc.scalar.activation(ds[t][:].indirect(n1_l[:]), pa[:, t % 2, :], COPY)
            for t in tiles:
                other = keep.tile([P, HALF], F32, name="other_a%d" % t, tag="other_a%d" % t)
                nc.scalar.activation(other[:], ds[t][:].indirect(entries(n3_l, 0, HALF)), COPY, scale=-0.5)
                add_transpose(t, ds[t][:, 0:HALF], True, False)
                add_transpose(t, other[:], False, True)
                if t == 1:
                    round_rows(0, 0, 2, zt_first[:, 0 : 2 * P])
                if t == 2:
                    round_rows(0, 2, 3, zt_first[:, 2 * P :])
        round_rows(0, TILES - 1, TILES, zt_last[:])

        other_b = keep.tile([P, TILES, HALF], F32, name="other_b", tag="late")
        for t in range(TILES):
            nc.scalar.activation(other_b[:, t, :], ds[t][:].indirect(entries(n3_l, HALF, HALF)), COPY, scale=-0.5)

        s_ps = [psum.tile([P, S], F32, name="s_ps%d" % t, tag="acc%d" % t) for t in range(TILES)]
        ds2 = [keep.tile([P, S], F32, name="ds2_%d" % t) for t in range(TILES)]
        for hf in range(2):
            cols = slice(hf * HALF, (hf + 1) * HALF)
            if hf == 1:
                z_first = keep.tile([P, TILES - 1, HALF], BF16, name="z_first", tag="other_a3")
                z_last = keep.tile([P, HALF], BF16, name="z_last", tag="zb0", align_bytes=64)
                z_b = [z_first[:, t, :] for t in range(TILES - 1)] + [z_last[:]]
                for t in range(TILES):
                    nc.vector.tensor_tensor(z_b[t], ds[t][:, HALF:S], other_b[:, t, :], ALU.add)
                zt_b = psum.tile([P, H], BF16, name="zt_b", tag="back0")
                for t in range(TILES):
                    nc.tensor.transpose(zt_b[:, t * P : (t + 1) * P], z_b[t], ident_bf[:])
                zb.append(keep.tile([P, 2, P, 2], BF16, name="zb1", tag="z_w0", align_bytes=64))
                round_rows(1, 0, TILES, zt_b[:])
            back = psum.tile([P, 2, HALF], F32, name="back%d" % hf, tag="back%d" % hf)
            words = zb[hf][:].rearrange("j u p e -> j (u p e)").bitcast(F32)
            for u in range(2):
                nc.tensor.transpose(back[:, u, :], words[:, u * P : (u + 1) * P], ident[:])
            z_in = keep.tile([P, HALF * PACK], BF16, name="z_in%d" % hf, align_bytes=64)
            nc.vector.tensor_copy(
                z_in[:].bitcast(F32).rearrange("p (j u) -> p j u", u=2), back[:].rearrange("p u j -> p j u")
            )
            z_w = keep.tile([P, HALF], U32, name="z_w%d" % hf, tag="z_w%d" % hf, align_bytes=64)
            z_sc = keep.tile([P, HALF], U8, name="z_sc%d" % hf, align_bytes=64)
            nc.vector.quantize_mx(out=z_w[:].bitcast(FP8X4), scales=z_sc[:], in_=z_in[:])
            for t in range(TILES):
                nc.tensor.matmul_mx(
                    out=s_ps[t][:, cols],
                    lhsT=c_w[:, t, :].bitcast(FP8X4),
                    lhsT_scale=c_plane[:, t * P : (t + 1) * P],
                    rhs=z_w[:].bitcast(FP8X4),
                    rhs_scale=z_sc[:],
                    start=True,
                    stop=True,
                )
                rl = keep.tile([P, HALF], F32, name="rl%d_%d" % (hf, t))
                nc.vector.tensor_scalar(rl[:], s_ps[t][:, cols], 0.0625, 0.0, ALU.mult, ALU.max)
                nc.scalar.activation(ds2[t][:].indirect(entries(n4_l, hf * HALF, HALF)), rl[:], COPY)

        y = keep.tile([P, TILES, S], F32, name="y")
        y_rows = out_0.rearrange("(p t) j -> p t j", t=PACK)
        for t in range(TILES):
            parts = (slice(0, S),) if t < TILES - 1 else (slice(0, HALF), slice(HALF, S))
            for cols in parts:
                nc.vector.scalar_tensor_tensor(
                    y[:, t, cols], s_ps[t][:, cols], -0.03125, ds2[t][:, cols], ALU.mult, ALU.add
                )
            nc.sync.dma_start(y_rows[:, t, :], y[:, t, :])

        y_w = keep.tile([P, S], U32, name="y_w", align_bytes=64)
        y_sc = keep.tile([P, S], U8, name="y_sc", align_bytes=64)
        y_in = [keep.tile([P, HALF * PACK], BF16, name="y_in%d" % hf, align_bytes=64) for hf in range(2)]
        for hf in range(2):
            cols = slice(hf * HALF, (hf + 1) * HALF)
            nc.vector.tensor_copy(
                y_in[hf][:].rearrange("p (c i t) -> p c t i", i=4, t=PACK),
                y[:, :, cols].rearrange("p t (c i) -> p c t i", i=4),
            )
        for hf in range(2):
            cols = slice(hf * HALF, (hf + 1) * HALF)
            nc.vector.quantize_mx(out=y_w[:, cols].bitcast(FP8X4), scales=y_sc[:, cols], in_=y_in[hf][:])
        nc.sync.dma_start(out_1[0].rearrange("p n t -> p (n t)").bitcast(I32), y_w[:].bitcast(I32))
        for q in range(4):
            queue = nc.scalar if q % 2 == 0 else nc.sync
            queue.dma_start(out_2[0, 4 * q : 4 * q + 4, :].bitcast(I32), y_sc[32 * q : 32 * q + 4, :].bitcast(I32))
